import numpy as np
import ml_dtypes


def mxq(x, axis, fmt="e4m3"):
    dtype, down = {"e4m3": (ml_dtypes.float8_e4m3fn, 7), "e5m2": (ml_dtypes.float8_e5m2, 14)}[fmt]
    v = np.moveaxis(np.asarray(x, np.float32).astype(ml_dtypes.bfloat16).astype(np.float64), axis, -1)
    blocks = v.reshape(v.shape[:-1] + (-1, 32))
    amax = np.abs(blocks).max(-1, keepdims=True)
    byte = np.maximum(np.where(amax > 0, np.frexp(amax)[1] - 1 + 127, 0) - down, 1)
    scale = np.exp2(byte - 127.0)
    codes = (blocks / scale).astype(np.float32).astype(dtype).astype(np.float64)
    return np.moveaxis((codes * scale).reshape(v.shape), -1, axis)


WIDE = False


def mx_kscale(k):
    if not WIDE:
        return np.ones(k)
    levels = np.array([10, -10, 5, -5, 0])
    if k % 512:
        return np.exp2(np.random.permutation(np.resize(levels, k // 32))).repeat(32)
    a = np.empty((k // 512, 16))
    for p in range(k // 512):
        a[p, :8] = np.random.permutation(np.resize(levels, 8))
        for g in range(8):
            far = levels[np.abs(levels - a[p, g]) >= 10]
            a[p, g + 8] = far[np.random.randint(len(far))]
    return np.exp2(a.ravel()).repeat(32)


BF16 = ml_dtypes.bfloat16


def bf(x):
    return np.asarray(x, np.float32).astype(BF16)


def f64(x):
    return np.asarray(x).astype(np.float64)


E2M1 = np.array([0.0, 0.5, 1.0, 1.5, 2.0, 3.0, 4.0, 6.0, -0.0, -0.5, -1.0, -1.5, -2.0, -3.0, -4.0, -6.0])


def pack_weight(w, fmt):
    k, n = w.shape
    w = f64(bf(w)).reshape(k // 32, 32, n)
    amax = np.abs(w).max(1)
    if fmt == "e4m3":
        byte = np.frexp(amax)[1] - 1 + 127 - 7
    else:
        mant, ex = np.frexp(amax / 6.0)
        byte = np.where(mant > 0.5, ex, ex - 1) + 127
    byte = np.clip(np.where(amax > 0, byte, 1), 1, 254)
    scaled = (w * np.exp2(127.0 - byte)[:, None, :]).reshape(k, n).astype(np.float32)
    by_word = np.ascontiguousarray(scaled.reshape(k // 512, 128, 4, n).transpose(0, 1, 3, 2))
    if fmt == "e4m3":
        words = by_word.astype(ml_dtypes.float8_e4m3fn).view(np.uint8)
    else:
        c = by_word.astype(ml_dtypes.float4_e2m1fn).view(np.uint8) & 0xF
        words = c[..., 0::2] | (c[..., 1::2] << 4)
    return np.ascontiguousarray(words), np.ascontiguousarray(byte.astype(np.uint8).reshape(k // 512, 16, n))


def unpack_weight(words, scales, fmt):
    g, p, n, _ = words.shape
    if fmt == "e4m3":
        vals = np.ascontiguousarray(words).view(ml_dtypes.float8_e4m3fn).astype(np.float64)
    else:
        nib = np.empty((g, p, n, 4), np.uint8)
        nib[..., 0::2] = words & 0xF
        nib[..., 1::2] = words >> 4
        vals = E2M1[nib]
    vals = vals * np.repeat(np.exp2(scales.astype(np.float64) - 127.0), 8, axis=1)[..., None]
    return vals.transpose(0, 1, 3, 2).reshape(g * 512, n)
def pack4(w):
    words, scales = pack_weight(w, "e2m1")
    return words.reshape(words.shape[0], 128, -1), scales


def unpack4(words, scales):
    return unpack_weight(words.reshape(words.shape[0], 128, -1, 2), scales, "e2m1")


G, M, K, N, R = 4, 768, 1024, 512, 512


def setup_inputs():
    s = mx_kscale(G * K)
    u = mx_kscale(G * K)
    t = mx_kscale(G * N)
    x = np.random.standard_normal((G, M, K)) * s.reshape(G, 1, K)
    y = np.random.standard_normal((G, M, K)) * u.reshape(G, 1, K)
    a = np.random.standard_normal((G * K, N)) / np.sqrt(2 * K) / s[:, None]
    b = np.random.standard_normal((G * K, N)) / np.sqrt(2 * K) / u[:, None]
    load = np.random.standard_normal((G * N, R)) / np.sqrt(N) / t[:, None]
    inv_var = (0.5 + np.random.random((G, N))) * t.reshape(G, N)
    a_words, a_scales = pack4(a)
    b_words, b_scales = pack4(b)
    load_words, load_scales = pack4(load)
    return {"x": bf(x), "y": bf(y), "inv_var": bf(inv_var),
            "a_words": a_words, "a_scales": a_scales,
            "b_words": b_words, "b_scales": b_scales,
            "load_words": load_words, "load_scales": load_scales}


def reference(x, y, inv_var, a_words, a_scales, b_words, b_scales, load_words, load_scales):
    a = unpack4(a_words, a_scales).reshape(G, K, N)
    b = unpack4(b_words, b_scales).reshape(G, K, N)
    load = unpack4(load_words, load_scales).reshape(G, N, R)
    d = (mxq(f64(x), 2, "e4m3") @ a) - (mxq(f64(y), 2, "e4m3") @ b)
    z = np.square(d) * f64(inv_var)[:, None, :]
    return mxq(z, 2, "e4m3") @ load

@@ -1,0 +1,294 @@
+from contextlib import ExitStack
+
+import concourse.mybir as mybir
+from concourse.masks import make_identity
+
+G, M, K, N, R = 4, 768, 1024, 512, 512
+FLOPS = G * (2 * 2 * M * K * N + 2 * M * N * R)
+
+F32 = mybir.dt.float32
+BF16 = mybir.dt.bfloat16
+I32 = mybir.dt.int32
+U32 = mybir.dt.uint32
+U8 = mybir.dt.uint8
+FP8X4 = mybir.dt.float8_e4m3fn_x4
+FP4X4 = mybir.dt.float4_e2m1fn_x4
+ALU = mybir.AluOpType
+ACT = mybir.ActivationFunctionType
+
+P = 128
+K_PASS = 512
+PASSES = K // K_PASS
+BANK = 512
+TILES_PER_GROUP = M // P
+TILES = G * TILES_PER_GROUP
+LOAD_AHEAD = 4
+
+
+def tile_grouped_alteration_detection_s14_kernel(
+    tc, x, y, inv_var, a_words, a_scales, b_words, b_scales, load_words, load_scales, out
+):
+    nc = tc.nc
+    steps = [[0], [1]] + [[t, t + 1] for t in range(2, TILES - 2, 2)] + [[TILES - 2], [TILES - 1]]
+    n_steps = len(steps)
+
+    def rows_of(tensor, tiles):
+        h, first = divmod(tiles[0], TILES_PER_GROUP)
+        pair, j = divmod(first, 2)
+        rows = tensor[h, 2 * P * pair : 2 * P * (pair + 1), :].rearrange("(p j) c -> p j c", j=2)
+        return rows[:, j : j + len(tiles), :]
+
+    with ExitStack() as ctx:
+        keep = ctx.enter_context(tc.tile_pool(name="keep", bufs=1))
+        raw_pool = ctx.enter_context(tc.tile_pool(name="raw", bufs=LOAD_AHEAD + 1))
+        work = ctx.enter_context(tc.tile_pool(name="work", bufs=3))
+        turn_banks = ctx.enter_context(tc.psum_pool(name="turn_banks", bufs=4))
+        sum_banks = ctx.enter_context(tc.psum_pool(name="sum_banks", bufs=4))
+        ctx.enter_context(tc.manual_schedule())
+
+        def scale_plane(name, passes):
+            plane = keep.tile([P, passes, N], U8, name=name, align_bytes=64)
+            nc.vector.memset(plane[:].bitcast(I32), 0)
+            return plane
+
+        def load_scales_into(queue, plane, scales, first, passes):
+            for q in range(4):
+                queue.dma_start(
+                    out=plane[32 * q : 32 * q + 4, :, :].bitcast(I32),
+                    in_=scales[first : first + passes, 4 * q : 4 * q + 4, :].rearrange("g r n -> r g n").bitcast(I32),
+                )
+
+        def load_words_of(name, words, first, passes):
+            codes = keep.tile([P, passes, 2 * N], U8, name=name, align_bytes=64)
+            nc.sync.dma_start(
+                out=codes[:].bitcast(I32),
+                in_=words[first : first + passes, :, :].rearrange("g p b -> p g b").bitcast(I32),
+            )
+            return codes
+
+        raw = {}
+
+        def load_rows(s):
+            for name, tensor in (("x", x), ("y", y)):
+                t = raw_pool.tile([P, len(steps[s]), K], BF16, name="raw_" + name, align_bytes=64)
+                nc.sync.dma_start(out=t[:], in_=rows_of(tensor, steps[s]))
+                raw[name, s] = t
+
+        a_plane0 = scale_plane("a_plane0", PASSES)
+        b_plane0 = scale_plane("b_plane0", PASSES)
+        l_plane = scale_plane("l_plane", G)
+        a_plane1 = scale_plane("a_plane1", (G - 1) * PASSES)
+        b_plane1 = scale_plane("b_plane1", (G - 1) * PASSES)
+
+        eye = keep.tile([P, P], F32, name="eye")
+        make_identity(nc, eye[:])
+        ident = keep.tile([P, P], F32, name="ident")
+        nc.scalar.activation(out=ident[:], in_=eye[:], func=ACT.Square)
+
+        a_codes, b_codes, l_codes = {}, {}, {}
+        load_rows(0)
+        gain_rows = keep.tile([P, G * N // P], BF16, name="gain_rows")
+        nc.sync.dma_start(out=gain_rows[:], in_=inv_var.rearrange("g (q j) -> (g q) j", j=G * N // P))
+        a_codes[0] = load_words_of("a_codes0", a_words, 0, PASSES)
+        load_scales_into(nc.sync, a_plane0, a_scales, 0, PASSES)
+        load_scales_into(nc.gpsimd, b_plane0, b_scales, 0, PASSES)
+        b_codes[0] = load_words_of("b_codes0", b_words, 0, PASSES)
+        load_rows(1)
+        load_rows(2)
+        l_codes[0] = load_words_of("l_codes0", load_words, 0, 1)
+        load_scales_into(nc.sync, l_plane, load_scales, 0, G)
+        load_rows(3)
+        load_scales_into(nc.sync, a_plane1, a_scales, PASSES, (G - 1) * PASSES)
+        load_scales_into(nc.sync, b_plane1, b_scales, PASSES, (G - 1) * PASSES)
+
+        def load_group(h):
+            a_codes[h] = load_words_of("a_codes%d" % h, a_words, h * PASSES, PASSES)
+            b_codes[h] = load_words_of("b_codes%d" % h, b_words, h * PASSES, PASSES)
+            l_codes[h] = load_words_of("l_codes%d" % h, load_words, h, 1)
+
+        def stage1_scales(plane0, plane1, h, g):
+            return plane0[:, g, :] if h == 0 else plane1[:, (h - 1) * PASSES + g, :]
+
+        gain = keep.tile([P, G, N], BF16, name="gain", align_bytes=64)
+
+        def spread_gain():
+            gain_words = gain_rows[:].bitcast(F32)
+            sorted_words = gain[:].bitcast(F32).rearrange("p h (u w) -> p h u w", u=2)
+            for u in range(2):
+                bank = sum_banks.tile([P, BANK], F32, name="sum_bank")
+                for c in range(4):
+                    j = 2 * c + u
+                    nc.tensor.transpose(
+                        bank[:, c * P : (c + 1) * P], gain_words[:, j : j + 1].to_broadcast([P, P]), ident[:]
+                    )
+                nc.scalar.copy(
+                    out=sorted_words[:, :, u, :].rearrange("p h (q c) -> p h q c", c=4),
+                    in_=bank[:].rearrange("p (c h q) -> p h q c", c=4, h=G),
+                )
+
+        pairs_sorted = {}
+
+        def sort_pairs(name, s):
+            width = len(steps[s]) * K
+            t = work.tile([P, width], BF16, name="sorted_" + name, align_bytes=64)
+            src = raw[name, s][:].rearrange("p j k -> p (j k)").rearrange("p (w u e) -> p u w e", u=2, e=2)
+            dst = t[:].rearrange("p (u w e) -> p u w e", u=2, e=2)
+            if name == "x":
+                nc.vector.tensor_copy(out=dst, in_=src)
+            else:
+                nc.vector.tensor_scalar(out=dst, in0=src, scalar1=-1.0, scalar2=None, op0=ALU.mult)
+            pairs_sorted[name, s] = t
+
+        turned = {}
+
+        def turn_inputs(s):
+            for j, i in enumerate(steps[s]):
+                for name in ("x", "y"):
+                    words = pairs_sorted[name, s][:].bitcast(F32).rearrange("p (u w) -> p u w", u=2)
+                    bank = turn_banks.tile([P, BANK], F32, name="turn_bank")
+                    for g in range(PASSES):
+                        for u in range(2):
+                            first = (j * PASSES + g) * P
+                            col = (g * 2 + u) * P
+                            nc.tensor.transpose(bank[:, col : col + P], words[:, u, first : first + P], ident[:])
+                    turned[name, i] = bank
+
+        def interleave(engine_copy, dst_bf16, bank):
+            engine_copy(
+                out=dst_bf16.bitcast(F32).rearrange("p (g m u) -> p g m u", u=2, m=P),
+                in_=bank.rearrange("p (g u m) -> p g m u", u=2, m=P),
+            )
+
+        grouped, in_codes, in_scales = {}, {}, {}
+
+        def copy_inputs(i):
+            t = work.tile([P, 2 * K], BF16, name="grouped", align_bytes=64)
+            interleave(nc.scalar.copy, t[:, :K], turned["x", i][:])
+            interleave(nc.scalar.copy, t[:, K:], turned["y", i][:])
+            grouped[i] = t
+
+        def quantize_inputs(i):
+            c = work.tile([P, 2 * PASSES * P], U32, name="in_codes", bufs=4, align_bytes=64)
+            sc = work.tile([P, 2 * PASSES * P], U8, name="in_scales", bufs=4, align_bytes=64)
+            nc.vector.quantize_mx(out=c[:].bitcast(FP8X4), scales=sc[:], in_=grouped[i][:])
+            in_codes[i], in_scales[i] = c, sc
+
+        diff, squares = {}, {}
+
+        def stage1(i):
+            h = i // TILES_PER_GROUP
+            bank = sum_banks.tile([P, BANK], F32, name="sum_bank")
+            weights = [(a_codes[h], a_plane0, a_plane1), (b_codes[h], b_plane0, b_plane1)]
+            for c in range(2 * PASSES):
+                codes, plane0, plane1 = weights[c // PASSES]
+                g = c % PASSES
+                cols = slice(c * P, (c + 1) * P)
+                nc.tensor.matmul_mx(
+                    out=bank[:],
+                    lhsT=in_codes[i][:, cols].bitcast(FP8X4),
+                    lhsT_scale=in_scales[i][:, cols],
+                    rhs=codes[:, g, :].bitcast(FP4X4),
+                    rhs_scale=stage1_scales(plane0, plane1, h, g),
+                    start=(c == 0),
+                    stop=(c == 2 * PASSES - 1),
+                )
+            diff[i] = bank
+
+        def square(i):
+            t = work.tile([P, N], F32, name="squares")
+            nc.scalar.activation(
+                out=t[:].rearrange("p (u w e) -> p u w e", u=2, e=2),
+                in_=diff[i][:].rearrange("p (w u e) -> p u w e", u=2, e=2),
+                func=ACT.Square,
+            )
+            squares[i] = t
+
+        z_rows, z_turned, z_grouped, z_codes, z_scales = {}, {}, {}, {}, {}
+
+        def scale_squares(i):
+            t = work.tile([P, N], BF16, name="z_rows", bufs=4, align_bytes=64)
+            nc.vector.tensor_tensor(out=t[:], in0=squares[i][:], in1=gain[:, i // TILES_PER_GROUP, :], op=ALU.mult)
+            z_rows[i] = t
+
+        def turn_z(s):
+            bank = sum_banks.tile([P, BANK], F32, name="sum_bank")
+            for j, i in enumerate(steps[s]):
+                words = z_rows[i][:].bitcast(F32)
+                for u in range(2):
+                    col = (j * 2 + u) * P
+                    nc.tensor.transpose(bank[:, col : col + P], words[:, u * P : (u + 1) * P], ident[:])
+            z_turned[s] = bank
+
+        def copy_z(s):
+            n = len(steps[s])
+            t = work.tile([P, n * N], BF16, name="z_grouped", align_bytes=64)
+            interleave(nc.vector.tensor_copy, t[:], z_turned[s][:, : n * 2 * P])
+            z_grouped[s] = t
+
+        def quantize_z(s):
+            n = len(steps[s])
+            c = work.tile([P, n * P], U32, name="z_codes", align_bytes=64)
+            sc = work.tile([P, n * P], U8, name="z_scales", align_bytes=64)
+            nc.vector.quantize_mx(out=c[:].bitcast(FP8X4), scales=sc[:], in_=z_grouped[s][:])
+            z_codes[s], z_scales[s] = c, sc
+
+        def stage2_and_store(s):
+            n = len(steps[s])
+            banks = []
+            for j, i in enumerate(steps[s]):
+                h = i // TILES_PER_GROUP
+                bank = sum_banks.tile([P, BANK], F32, name="sum_bank")
+                cols = slice(j * P, (j + 1) * P)
+                nc.tensor.matmul_mx(
+                    out=bank[:],
+                    lhsT=z_codes[s][:, cols].bitcast(FP8X4),
+                    lhsT_scale=z_scales[s][:, cols],
+                    rhs=l_codes[h][:, 0, :].bitcast(FP4X4),
+                    rhs_scale=l_plane[:, h, :],
+                    start=True,
+                    stop=True,
+                )
+                banks.append(bank)
+            result = work.tile([P, n, R], F32, name="result")
+            for j in range(n):
+                nc.scalar.copy(out=result[:, j, :], in_=banks[j][:])
+            nc.sync.dma_start(out=rows_of(out, steps[s]), in_=result[:])
+
+        sort_pairs("x", 0)
+        sort_pairs("y", 0)
+        for s in range(n_steps + 2):
+            now = steps[s] if s < n_steps else []
+            before = steps[s - 1] if 1 <= s <= n_steps else []
+            ahead = s + LOAD_AHEAD
+            if ahead < n_steps:
+                h, first = divmod(steps[ahead][0], TILES_PER_GROUP)
+                if first == 0:
+                    load_group(h)
+                load_rows(ahead)
+            if s >= 2:
+                scale_squares(steps[s - 2][-1])
+            if now:
+                turn_inputs(s)
+            if s + 1 < n_steps:
+                sort_pairs("x", s + 1)
+                sort_pairs("y", s + 1)
+            if s >= 2:
+                turn_z(s - 2)
+                copy_z(s - 2)
+            for i in now:
+                copy_inputs(i)
+            if s == 0:
+                spread_gain()
+            if now:
+                quantize_inputs(now[0])
+            if s >= 2:
+                quantize_z(s - 2)
+            for i in now[1:]:
+                quantize_inputs(i)
+            for i in before:
+                stage1(i)
+                square(i)
+            for i in before[:-1]:
+                scale_squares(i)
+            if s >= 2:
+                stage2_and_store(s - 2)

@@ -22,15 +22,26 @@ PASSES = K // K_PASS
 BANK = 512
 TILES_PER_GROUP = M // P
 TILES = G * TILES_PER_GROUP
-LOAD_AHEAD = 4
+LOAD_AHEAD = 5
+TURN_BANKS = 3
+STAGE1_LAG = 2
+V_TAIL = 3
+S2_OFF = 1
+SINGLES = 4
+RAMP = 3
+TAIL_FROM = 25
+TAIL_OFF = 1
 
 
 def tile_grouped_alteration_detection_s14_kernel(
     tc, x, y, inv_var, a_words, a_scales, b_words, b_scales, load_words, load_scales, out
 ):
     nc = tc.nc
-    steps = [[0], [1]] + [[t, t + 1] for t in range(2, TILES - 2, 2)] + [[TILES - 2], [TILES - 1]]
+    steps = [[t] for t in range(SINGLES)] + [[t, t + 1] for t in range(SINGLES, TILES, 2)]
     n_steps = len(steps)
+    units = [[t, t + 1] for t in range(0, TILES - 2, 2)] + [[TILES - 2], [TILES - 1]]
+    step_of = {i: (s, j) for s, tiles in enumerate(steps) for j, i in enumerate(tiles)}
+    unit_of = {i: (s, j) for s, tiles in enumerate(units) for j, i in enumerate(tiles)}
 
     def rows_of(tensor, tiles):
         h, first = divmod(tiles[0], TILES_PER_GROUP)
@@ -42,8 +53,8 @@ def tile_grouped_alteration_detection_s14_kernel(
         keep = ctx.enter_context(tc.tile_pool(name="keep", bufs=1))
         raw_pool = ctx.enter_context(tc.tile_pool(name="raw", bufs=LOAD_AHEAD + 1))
         work = ctx.enter_context(tc.tile_pool(name="work", bufs=3))
-        turn_banks = ctx.enter_context(tc.psum_pool(name="turn_banks", bufs=4))
-        sum_banks = ctx.enter_context(tc.psum_pool(name="sum_banks", bufs=4))
+        turn_banks = ctx.enter_context(tc.psum_pool(name="turn_banks", bufs=TURN_BANKS))
+        sum_banks = ctx.enter_context(tc.psum_pool(name="sum_banks", bufs=8 - TURN_BANKS))
         ctx.enter_context(tc.manual_schedule())
 
         def scale_plane(name, passes):
@@ -68,11 +79,14 @@ def tile_grouped_alteration_detection_s14_kernel(
 
         raw = {}
 
+        def load_rows_of(name, s):
+            t = raw_pool.tile([P, len(steps[s]), K], BF16, name="raw_" + name, align_bytes=64)
+            nc.sync.dma_start(out=t[:], in_=rows_of(x if name == "x" else y, steps[s]))
+            raw[name, s] = t
+
         def load_rows(s):
-            for name, tensor in (("x", x), ("y", y)):
-                t = raw_pool.tile([P, len(steps[s]), K], BF16, name="raw_" + name, align_bytes=64)
-                nc.sync.dma_start(out=t[:], in_=rows_of(tensor, steps[s]))
-                raw[name, s] = t
+            load_rows_of("x", s)
+            load_rows_of("y", s)
 
         a_plane0 = scale_plane("a_plane0", PASSES)
         b_plane0 = scale_plane("b_plane0", PASSES)
@@ -82,24 +96,24 @@ def tile_grouped_alteration_detection_s14_kernel(
 
         eye = keep.tile([P, P], F32, name="eye")
         make_identity(nc, eye[:])
-        ident = keep.tile([P, P], F32, name="ident")
-        nc.scalar.activation(out=ident[:], in_=eye[:], func=ACT.Square)
 
         a_codes, b_codes, l_codes = {}, {}, {}
+        load_scales_into(nc.scalar, a_plane0, a_scales, 0, PASSES)
+        ident = keep.tile([P, P], F32, name="ident")
+        nc.scalar.activation(out=ident[:], in_=eye[:], func=ACT.Square)
         load_rows(0)
+        load_rows_of("x", 1)
         gain_rows = keep.tile([P, G * N // P], BF16, name="gain_rows")
         nc.sync.dma_start(out=gain_rows[:], in_=inv_var.rearrange("g (q j) -> (g q) j", j=G * N // P))
         a_codes[0] = load_words_of("a_codes0", a_words, 0, PASSES)
-        load_scales_into(nc.sync, a_plane0, a_scales, 0, PASSES)
-        load_scales_into(nc.gpsimd, b_plane0, b_scales, 0, PASSES)
+        load_rows_of("y", 1)
         b_codes[0] = load_words_of("b_codes0", b_words, 0, PASSES)
-        load_rows(1)
+        load_scales_into(nc.sync, b_plane0, b_scales, 0, PASSES)
         load_rows(2)
+        load_rows(3)
+        load_rows(4)
         l_codes[0] = load_words_of("l_codes0", load_words, 0, 1)
         load_scales_into(nc.sync, l_plane, load_scales, 0, G)
-        load_rows(3)
-        load_scales_into(nc.sync, a_plane1, a_scales, PASSES, (G - 1) * PASSES)
-        load_scales_into(nc.sync, b_plane1, b_scales, PASSES, (G - 1) * PASSES)
 
         def load_group(h):
             a_codes[h] = load_words_of("a_codes%d" % h, a_words, h * PASSES, PASSES)
@@ -111,9 +125,10 @@ def tile_grouped_alteration_detection_s14_kernel(
 
         gain = keep.tile([P, G, N], BF16, name="gain", align_bytes=64)
 
-        def spread_gain():
+        gain_banks = []
+
+        def spread_gain_turn():
             gain_words = gain_rows[:].bitcast(F32)
-            sorted_words = gain[:].bitcast(F32).rearrange("p h (u w) -> p h u w", u=2)
             for u in range(2):
                 bank = sum_banks.tile([P, BANK], F32, name="sum_bank")
                 for c in range(4):
@@ -121,6 +136,11 @@ def tile_grouped_alteration_detection_s14_kernel(
                     nc.tensor.transpose(
                         bank[:, c * P : (c + 1) * P], gain_words[:, j : j + 1].to_broadcast([P, P]), ident[:]
                     )
+                gain_banks.append(bank)
+
+        def spread_gain_copy():
+            sorted_words = gain[:].bitcast(F32).rearrange("p h (u w) -> p h u w", u=2)
+            for u, bank in enumerate(gain_banks):
                 nc.scalar.copy(
                     out=sorted_words[:, :, u, :].rearrange("p h (q c) -> p h q c", c=4),
                     in_=bank[:].rearrange("p (c h q) -> p h q c", c=4, h=G),
@@ -141,17 +161,17 @@ def tile_grouped_alteration_detection_s14_kernel(
 
         turned = {}
 
-        def turn_inputs(s):
-            for j, i in enumerate(steps[s]):
-                for name in ("x", "y"):
-                    words = pairs_sorted[name, s][:].bitcast(F32).rearrange("p (u w) -> p u w", u=2)
-                    bank = turn_banks.tile([P, BANK], F32, name="turn_bank")
-                    for g in range(PASSES):
-                        for u in range(2):
-                            first = (j * PASSES + g) * P
-                            col = (g * 2 + u) * P
-                            nc.tensor.transpose(bank[:, col : col + P], words[:, u, first : first + P], ident[:])
-                    turned[name, i] = bank
+        def turn_inputs(i):
+            s, j = step_of[i]
+            for name in ("x", "y"):
+                words = pairs_sorted[name, s][:].bitcast(F32).rearrange("p (u w) -> p u w", u=2)
+                bank = turn_banks.tile([P, BANK], F32, name="turn_bank")
+                for g in range(PASSES):
+                    for u in range(2):
+                        first = (j * PASSES + g) * P
+                        col = (g * 2 + u) * P
+                        nc.tensor.transpose(bank[:, col : col + P], words[:, u, first : first + P], ident[:])
+                turned[name, i] = bank
 
         def interleave(engine_copy, dst_bf16, bank):
             engine_copy(
@@ -164,7 +184,7 @@ def tile_grouped_alteration_detection_s14_kernel(
         def copy_inputs(i):
             t = work.tile([P, 2 * K], BF16, name="grouped", align_bytes=64)
             interleave(nc.scalar.copy, t[:, :K], turned["x", i][:])
-            interleave(nc.scalar.copy, t[:, K:], turned["y", i][:])
+            interleave(nc.vector.tensor_copy if i == 0 else nc.scalar.copy, t[:, K:], turned["y", i][:])
             grouped[i] = t
 
         def quantize_inputs(i):
@@ -212,7 +232,7 @@ def tile_grouped_alteration_detection_s14_kernel(
 
         def turn_z(s):
             bank = sum_banks.tile([P, BANK], F32, name="sum_bank")
-            for j, i in enumerate(steps[s]):
+            for j, i in enumerate(units[s]):
                 words = z_rows[i][:].bitcast(F32)
                 for u in range(2):
                     col = (j * 2 + u) * P
@@ -220,75 +240,98 @@ def tile_grouped_alteration_detection_s14_kernel(
             z_turned[s] = bank
 
         def copy_z(s):
-            n = len(steps[s])
+            n = len(units[s])
             t = work.tile([P, n * N], BF16, name="z_grouped", align_bytes=64)
             interleave(nc.vector.tensor_copy, t[:], z_turned[s][:, : n * 2 * P])
             z_grouped[s] = t
 
         def quantize_z(s):
-            n = len(steps[s])
+            n = len(units[s])
             c = work.tile([P, n * P], U32, name="z_codes", align_bytes=64)
             sc = work.tile([P, n * P], U8, name="z_scales", align_bytes=64)
             nc.vector.quantize_mx(out=c[:].bitcast(FP8X4), scales=sc[:], in_=z_grouped[s][:])
             z_codes[s], z_scales[s] = c, sc
 
-        def stage2_and_store(s):
-            n = len(steps[s])
-            banks = []
-            for j, i in enumerate(steps[s]):
-                h = i // TILES_PER_GROUP
-                bank = sum_banks.tile([P, BANK], F32, name="sum_bank")
-                cols = slice(j * P, (j + 1) * P)
-                nc.tensor.matmul_mx(
-                    out=bank[:],
-                    lhsT=z_codes[s][:, cols].bitcast(FP8X4),
-                    lhsT_scale=z_scales[s][:, cols],
-                    rhs=l_codes[h][:, 0, :].bitcast(FP4X4),
-                    rhs_scale=l_plane[:, h, :],
-                    start=True,
-                    stop=True,
-                )
-                banks.append(bank)
-            result = work.tile([P, n, R], F32, name="result")
-            for j in range(n):
-                nc.scalar.copy(out=result[:, j, :], in_=banks[j][:])
-            nc.sync.dma_start(out=rows_of(out, steps[s]), in_=result[:])
+        scores, results = {}, {}
+
+        def stage2(i):
+            s, j = unit_of[i]
+            h = i // TILES_PER_GROUP
+            bank = sum_banks.tile([P, BANK], F32, name="sum_bank")
+            cols = slice(j * P, (j + 1) * P)
+            nc.tensor.matmul_mx(
+                out=bank[:],
+                lhsT=z_codes[s][:, cols].bitcast(FP8X4),
+                lhsT_scale=z_scales[s][:, cols],
+                rhs=l_codes[h][:, 0, :].bitcast(FP4X4),
+                rhs_scale=l_plane[:, h, :],
+                start=True,
+                stop=True,
+            )
+            scores[i] = bank
+
+        def copy_and_store(i):
+            s, j = unit_of[i]
+            if j == 0:
+                results[s] = work.tile([P, len(units[s]), R], F32, name="result", bufs=4)
+            copy = nc.vector.tensor_copy if i >= TILES - V_TAIL and i != TILES - 2 else nc.scalar.copy
+            copy(out=results[s][:, j, :], in_=scores[i][:])
+            if j == len(units[s]) - 1:
+                nc.sync.dma_start(out=rows_of(out, units[s]), in_=results[s][:])
+
+        stage1_at = {i: i + (1 if i < RAMP else STAGE1_LAG) for i in range(TILES)}
+        stage1_slot = {t: i for i, t in enumerate([stage1_at[i] for i in range(TILES)])}
+        z_slot = {stage1_at[tiles[-1]] + 2: s for s, tiles in enumerate(units)}
+        stage2_slot = {}
+        for tiles in units:
+            for j, i in enumerate(tiles):
+                z_at = stage1_at[tiles[-1]] + 2
+                stage2_slot.setdefault(z_at + S2_OFF + j if z_at < TAIL_FROM else z_at + TAIL_OFF, []).append(i)
+        sort_slot = {}
+        for s in range(1, n_steps):
+            first = steps[s][0]
+            sort_slot.setdefault(first - len(steps[s - 1]), []).append(("x", s))
+            sort_slot.setdefault(first - 1, []).append(("y", s))
 
         sort_pairs("x", 0)
         sort_pairs("y", 0)
-        for s in range(n_steps + 2):
-            now = steps[s] if s < n_steps else []
-            before = steps[s - 1] if 1 <= s <= n_steps else []
-            ahead = s + LOAD_AHEAD
-            if ahead < n_steps:
+        for t in range(TILES + STAGE1_LAG + 5):
+            if t < TILES and step_of[t][1] == 0 and step_of[t][0] + LOAD_AHEAD < n_steps:
+                ahead = step_of[t][0] + LOAD_AHEAD
                 h, first = divmod(steps[ahead][0], TILES_PER_GROUP)
+                load_rows_of("x", ahead)
+                load_rows_of("y", ahead)
                 if first == 0:
                     load_group(h)
-                load_rows(ahead)
-            if s >= 2:
-                scale_squares(steps[s - 2][-1])
-            if now:
-                turn_inputs(s)
-            if s + 1 < n_steps:
-                sort_pairs("x", s + 1)
-                sort_pairs("y", s + 1)
-            if s >= 2:
-                turn_z(s - 2)
-                copy_z(s - 2)
-            for i in now:
-                copy_inputs(i)
-            if s == 0:
-                spread_gain()
-            if now:
-                quantize_inputs(now[0])
-            if s >= 2:
-                quantize_z(s - 2)
-            for i in now[1:]:
-                quantize_inputs(i)
-            for i in before:
-                stage1(i)
-                square(i)
-            for i in before[:-1]:
-                scale_squares(i)
-            if s >= 2:
-                stage2_and_store(s - 2)
+                    if h == 1:
+                        load_scales_into(nc.sync, a_plane1, a_scales, PASSES, (G - 1) * PASSES)
+                if first == 2 and h == 1:
+                    load_scales_into(nc.sync, b_plane1, b_scales, PASSES, (G - 1) * PASSES)
+            if t in z_slot:
+                turn_z(z_slot[t])
+                copy_z(z_slot[t])
+            if t - 1 in stage1_slot:
+                scale_squares(stage1_slot[t - 1])
+            if t in z_slot:
+                quantize_z(z_slot[t])
+            if t < TILES:
+                turn_inputs(t)
+            if t == 0:
+                spread_gain_turn()
+                sort_pairs("x", 1)
+                copy_inputs(0)
+                spread_gain_copy()
+                sort_pairs("y", 1)
+                quantize_inputs(0)
+            for name, s in sort_slot.get(t, []) if t > 0 else []:
+                sort_pairs(name, s)
+            if 0 < t < TILES:
+                copy_inputs(t)
+                quantize_inputs(t)
+            for i in stage2_slot.get(t - 1, []):
+                copy_and_store(i)
+            if t in stage1_slot:
+                stage1(stage1_slot[t])
+                square(stage1_slot[t])
+            for i in stage2_slot.get(t, []):
+                stage2(i)

@@ -23,14 +23,17 @@ BANK = 512
 TILES_PER_GROUP = M // P
 TILES = G * TILES_PER_GROUP
 LOAD_AHEAD = 5
-TURN_BANKS = 3
+TURN_BANKS = 4
 STAGE1_LAG = 2
 V_TAIL = 3
 S2_OFF = 1
 SINGLES = 4
-RAMP = 3
+KEEP = 0
+STORE1 = 20
+RAMP = 4
 TAIL_FROM = 25
 TAIL_OFF = 1
+GAIN_SLOT = 1
 
 
 def tile_grouped_alteration_detection_s14_kernel(
@@ -154,7 +157,10 @@ def tile_grouped_alteration_detection_s14_kernel(
             src = raw[name, s][:].rearrange("p j k -> p (j k)").rearrange("p (w u e) -> p u w e", u=2, e=2)
             dst = t[:].rearrange("p (u w e) -> p u w e", u=2, e=2)
             if name == "x":
-                nc.vector.tensor_copy(out=dst, in_=src)
+                nc.vector.tensor_copy(
+                    out=t[:].bitcast(F32).rearrange("p (u w) -> p u w", u=2),
+                    in_=raw[name, s][:].rearrange("p j k -> p (j k)").bitcast(F32).rearrange("p (w u) -> p u w", u=2),
+                )
             else:
                 nc.vector.tensor_scalar(out=dst, in0=src, scalar1=-1.0, scalar2=None, op0=ALU.mult)
             pairs_sorted[name, s] = t
@@ -270,68 +276,115 @@ def tile_grouped_alteration_detection_s14_kernel(
             )
             scores[i] = bank
 
-        def copy_and_store(i):
+        def copy_and_store(i, copy):
             s, j = unit_of[i]
             if j == 0:
                 results[s] = work.tile([P, len(units[s]), R], F32, name="result", bufs=4)
-            copy = nc.vector.tensor_copy if i >= TILES - V_TAIL and i != TILES - 2 else nc.scalar.copy
             copy(out=results[s][:, j, :], in_=scores[i][:])
-            if j == len(units[s]) - 1:
+            if i >= STORE1:
+                nc.sync.dma_start(out=rows_of(out, [i]), in_=results[s][:, j : j + 1, :])
+            elif j == len(units[s]) - 1:
                 nc.sync.dma_start(out=rows_of(out, units[s]), in_=results[s][:])
 
-        stage1_at = {i: i + (1 if i < RAMP else STAGE1_LAG) for i in range(TILES)}
-        stage1_slot = {t: i for i, t in enumerate([stage1_at[i] for i in range(TILES)])}
-        z_slot = {stage1_at[tiles[-1]] + 2: s for s, tiles in enumerate(units)}
-        stage2_slot = {}
-        for tiles in units:
-            for j, i in enumerate(tiles):
-                z_at = stage1_at[tiles[-1]] + 2
-                stage2_slot.setdefault(z_at + S2_OFF + j if z_at < TAIL_FROM else z_at + TAIL_OFF, []).append(i)
-        sort_slot = {}
-        for s in range(1, n_steps):
-            first = steps[s][0]
-            sort_slot.setdefault(first - len(steps[s - 1]), []).append(("x", s))
-            sort_slot.setdefault(first - 1, []).append(("y", s))
-
-        sort_pairs("x", 0)
-        sort_pairs("y", 0)
-        for t in range(TILES + STAGE1_LAG + 5):
-            if t < TILES and step_of[t][1] == 0 and step_of[t][0] + LOAD_AHEAD < n_steps:
-                ahead = step_of[t][0] + LOAD_AHEAD
+        def load_ahead(s):
+            ahead = s + LOAD_AHEAD
+            if ahead < n_steps:
                 h, first = divmod(steps[ahead][0], TILES_PER_GROUP)
-                load_rows_of("x", ahead)
-                load_rows_of("y", ahead)
+                load_rows(ahead)
                 if first == 0:
                     load_group(h)
                     if h == 1:
                         load_scales_into(nc.sync, a_plane1, a_scales, PASSES, (G - 1) * PASSES)
                 if first == 2 and h == 1:
                     load_scales_into(nc.sync, b_plane1, b_scales, PASSES, (G - 1) * PASSES)
-            if t in z_slot:
-                turn_z(z_slot[t])
-                copy_z(z_slot[t])
-            if t - 1 in stage1_slot:
-                scale_squares(stage1_slot[t - 1])
-            if t in z_slot:
-                quantize_z(z_slot[t])
-            if t < TILES:
-                turn_inputs(t)
-            if t == 0:
-                spread_gain_turn()
-                sort_pairs("x", 1)
-                copy_inputs(0)
-                spread_gain_copy()
-                sort_pairs("y", 1)
-                quantize_inputs(0)
-            for name, s in sort_slot.get(t, []) if t > 0 else []:
-                sort_pairs(name, s)
-            if 0 < t < TILES:
-                copy_inputs(t)
-                quantize_inputs(t)
-            for i in stage2_slot.get(t - 1, []):
-                copy_and_store(i)
-            if t in stage1_slot:
-                stage1(stage1_slot[t])
-                square(stage1_slot[t])
-            for i in stage2_slot.get(t, []):
-                stage2(i)
+
+        on_scalar, on_vector = nc.scalar.copy, nc.vector.tensor_copy
+
+        load_ahead(0)
+        sort_pairs("x", 0)
+        sort_pairs("y", 0)
+        turn_inputs(0)
+        spread_gain_turn()
+        sort_pairs("x", 1)
+        copy_inputs(0)
+        spread_gain_copy()
+        sort_pairs("y", 1)
+        quantize_inputs(0)
+        for s in range(1, SINGLES):
+            load_ahead(s)
+            turn_inputs(s)
+            if s >= 2:
+                scale_squares(s - 2)
+            sort_pairs("x", s + 1)
+            sort_pairs("y", s + 1)
+            copy_inputs(s)
+            quantize_inputs(s)
+            stage1(s - 1)
+            square(s - 1)
+
+        last = n_steps - 1
+        for s in range(SINGLES, n_steps):
+            a, b = steps[s]
+            before = steps[s - 1]
+            unit = a // 2 - 2
+            load_ahead(s)
+            if s == SINGLES:
+                turn_z(unit)
+                copy_z(unit)
+            scale_squares(before[0] - 1)
+            if s == SINGLES:
+                quantize_z(unit)
+            turn_inputs(a)
+            turn_inputs(b)
+            if s < last:
+                sort_pairs("x", s + 1)
+                sort_pairs("y", s + 1)
+            if s > SINGLES:
+                turn_z(unit)
+                copy_z(unit)
+            copy_inputs(a)
+            copy_inputs(b)
+            quantize_inputs(a)
+            if s > SINGLES:
+                quantize_z(unit)
+            quantize_inputs(b)
+            for i in before:
+                stage1(i)
+                square(i)
+            for i in before[:-1]:
+                scale_squares(i)
+            if s < last + KEEP:
+                for i in units[unit]:
+                    stage2(i)
+                for i in units[unit]:
+                    copy_and_store(i, on_scalar)
+
+        a, b = steps[last]
+        scale_squares(a - 1)
+        stage1(a)
+        square(a)
+        stage1(b)
+        turn_z(a // 2 - 1)
+        scale_squares(a)
+        copy_z(a // 2 - 1)
+        square(b)
+        stage2(a - 4)
+        stage2(a - 3)
+        turn_z(a // 2)
+        scale_squares(b)
+        quantize_z(a // 2 - 1)
+        copy_and_store(a - 4, on_scalar)
+        copy_and_store(a - 3, on_scalar)
+        copy_z(a // 2)
+        turn_z(a // 2 + 1)
+        stage2(a - 2)
+        stage2(a - 1)
+        copy_z(a // 2 + 1)
+        quantize_z(a // 2)
+        quantize_z(a // 2 + 1)
+        stage2(a)
+        stage2(b)
+        copy_and_store(a - 2, on_scalar)
+        copy_and_store(a - 1, on_vector)
+        copy_and_store(a, on_scalar)
+        copy_and_store(b, on_vector)

@@ -22,155 +22,151 @@ PASSES = K // K_PASS
 BANK = 512
 TILES_PER_GROUP = M // P
 TILES = G * TILES_PER_GROUP
+SINGLE_STEPS = 4
 LOAD_AHEAD = 5
-TURN_BANKS = 4
-STAGE1_LAG = 2
-V_TAIL = 3
-S2_OFF = 1
-SINGLES = 4
-KEEP = 0
-STORE1 = 20
-RAMP = 4
-TAIL_FROM = 25
-TAIL_OFF = 1
-GAIN_SLOT = 1
+SINGLE_STORES_FROM = TILES - 6
 
 
 def tile_grouped_alteration_detection_s14_kernel(
     tc, x, y, inv_var, a_words, a_scales, b_words, b_scales, load_words, load_scales, out
 ):
     nc = tc.nc
-    steps = [[t] for t in range(SINGLES)] + [[t, t + 1] for t in range(SINGLES, TILES, 2)]
-    n_steps = len(steps)
-    units = [[t, t + 1] for t in range(0, TILES - 2, 2)] + [[TILES - 2], [TILES - 1]]
-    step_of = {i: (s, j) for s, tiles in enumerate(steps) for j, i in enumerate(tiles)}
-    unit_of = {i: (s, j) for s, tiles in enumerate(units) for j, i in enumerate(tiles)}
+    on_scalar, on_vector = nc.scalar.copy, nc.vector.tensor_copy
 
-    def rows_of(tensor, tiles):
-        h, first = divmod(tiles[0], TILES_PER_GROUP)
-        pair, j = divmod(first, 2)
+    steps = [[i] for i in range(SINGLE_STEPS)] + [[i, i + 1] for i in range(SINGLE_STEPS, TILES, 2)]
+    last_step = len(steps) - 1
+    step_of = {i: (s, j) for s, tiles in enumerate(steps) for j, i in enumerate(tiles)}
+    batches = [[0]] + [[i, i + 1] for i in range(1, TILES - 3, 2)] + [[i] for i in range(TILES - 3, TILES)]
+    batch_of = {i: (z, j) for z, tiles in enumerate(batches) for j, i in enumerate(tiles)}
+
+    def rows_of(tensor, first_tile, count):
+        h, in_group = divmod(first_tile, TILES_PER_GROUP)
+        pair, j = divmod(in_group, 2)
         rows = tensor[h, 2 * P * pair : 2 * P * (pair + 1), :].rearrange("(p j) c -> p j c", j=2)
-        return rows[:, j : j + len(tiles), :]
+        return rows[:, j : j + count, :]
 
     with ExitStack() as ctx:
         keep = ctx.enter_context(tc.tile_pool(name="keep", bufs=1))
         raw_pool = ctx.enter_context(tc.tile_pool(name="raw", bufs=LOAD_AHEAD + 1))
         work = ctx.enter_context(tc.tile_pool(name="work", bufs=3))
-        turn_banks = ctx.enter_context(tc.psum_pool(name="turn_banks", bufs=TURN_BANKS))
-        sum_banks = ctx.enter_context(tc.psum_pool(name="sum_banks", bufs=8 - TURN_BANKS))
+        turn_banks = ctx.enter_context(tc.psum_pool(name="turn_banks", bufs=4))
+        sum_banks = ctx.enter_context(tc.psum_pool(name="sum_banks", bufs=4))
         ctx.enter_context(tc.manual_schedule())
 
-        def scale_plane(name, passes):
-            plane = keep.tile([P, passes, N], U8, name=name, align_bytes=64)
-            nc.vector.memset(plane[:].bitcast(I32), 0)
-            return plane
 
-        def load_scales_into(queue, plane, scales, first, passes):
+        def scale_tile(name, passes):
+            t = keep.tile([P, passes, N], U8, name=name, align_bytes=64)
+            nc.vector.memset(t[:].bitcast(I32), 0)
+            return t
+
+        def load_scale_rows(queue, t, scales, first_pass, passes):
             for q in range(4):
+                rows = scales[first_pass : first_pass + passes, 4 * q : 4 * q + 4, :]
                 queue.dma_start(
-                    out=plane[32 * q : 32 * q + 4, :, :].bitcast(I32),
-                    in_=scales[first : first + passes, 4 * q : 4 * q + 4, :].rearrange("g r n -> r g n").bitcast(I32),
+                    out=t[32 * q : 32 * q + 4, :, :].bitcast(I32), in_=rows.rearrange("g r n -> r g n").bitcast(I32)
                 )
 
-        def load_words_of(name, words, first, passes):
-            codes = keep.tile([P, passes, 2 * N], U8, name=name, align_bytes=64)
-            nc.sync.dma_start(
-                out=codes[:].bitcast(I32),
-                in_=words[first : first + passes, :, :].rearrange("g p b -> p g b").bitcast(I32),
-            )
-            return codes
+        def load_codes(name, words, first_pass, passes):
+            t = keep.tile([P, passes, 2 * N], U8, name=name, align_bytes=64)
+            rows = words[first_pass : first_pass + passes, :, :]
+            nc.sync.dma_start(out=t[:].bitcast(I32), in_=rows.rearrange("g p b -> p g b").bitcast(I32))
+            return t
 
-        raw = {}
+        raw, a_codes, b_codes, l_codes = {}, {}, {}, {}
 
-        def load_rows_of(name, s):
-            t = raw_pool.tile([P, len(steps[s]), K], BF16, name="raw_" + name, align_bytes=64)
-            nc.sync.dma_start(out=t[:], in_=rows_of(x if name == "x" else y, steps[s]))
-            raw[name, s] = t
+        def load_rows(name, s):
+            count = len(steps[s])
+            raw[name, s] = raw_pool.tile([P, count, K], BF16, name="raw_" + name, align_bytes=64)
+            nc.sync.dma_start(out=raw[name, s][:], in_=rows_of(x if name == "x" else y, steps[s][0], count))
 
-        def load_rows(s):
-            load_rows_of("x", s)
-            load_rows_of("y", s)
+        def preload_for(s):
+            ahead = s + LOAD_AHEAD
+            if ahead > last_step:
+                return
+            load_rows("x", ahead)
+            load_rows("y", ahead)
+            h, in_group = divmod(steps[ahead][0], TILES_PER_GROUP)
+            if in_group == 0:
+                a_codes[h] = load_codes("a_codes%d" % h, a_words, h * PASSES, PASSES)
+                b_codes[h] = load_codes("b_codes%d" % h, b_words, h * PASSES, PASSES)
+                l_codes[h] = load_codes("l_codes%d" % h, load_words, h, 1)
+            if steps[ahead][0] == TILES_PER_GROUP:
+                load_scale_rows(nc.sync, a_scales_rest, a_scales, PASSES, (G - 1) * PASSES)
+            if steps[ahead][0] == TILES_PER_GROUP + 2:
+                load_scale_rows(nc.sync, b_scales_rest, b_scales, PASSES, (G - 1) * PASSES)
 
-        a_plane0 = scale_plane("a_plane0", PASSES)
-        b_plane0 = scale_plane("b_plane0", PASSES)
-        l_plane = scale_plane("l_plane", G)
-        a_plane1 = scale_plane("a_plane1", (G - 1) * PASSES)
-        b_plane1 = scale_plane("b_plane1", (G - 1) * PASSES)
+        a_scales_first = scale_tile("a_scales_first", PASSES)
+        b_scales_first = scale_tile("b_scales_first", PASSES)
+        l_scales = scale_tile("l_scales", G)
+        a_scales_rest = scale_tile("a_scales_rest", (G - 1) * PASSES)
+        b_scales_rest = scale_tile("b_scales_rest", (G - 1) * PASSES)
 
-        eye = keep.tile([P, P], F32, name="eye")
-        make_identity(nc, eye[:])
-
-        a_codes, b_codes, l_codes = {}, {}, {}
-        load_scales_into(nc.scalar, a_plane0, a_scales, 0, PASSES)
         ident = keep.tile([P, P], F32, name="ident")
-        nc.scalar.activation(out=ident[:], in_=eye[:], func=ACT.Square)
-        load_rows(0)
-        load_rows_of("x", 1)
+        make_identity(nc, ident[:])
+
+        load_scale_rows(nc.scalar, a_scales_first, a_scales, 0, PASSES)
+        z_ident = keep.tile([P, P], F32, name="z_ident")
+        nc.scalar.activation(out=z_ident[:], in_=ident[:], func=ACT.Square)
+
         gain_rows = keep.tile([P, G * N // P], BF16, name="gain_rows")
-        nc.sync.dma_start(out=gain_rows[:], in_=inv_var.rearrange("g (q j) -> (g q) j", j=G * N // P))
-        a_codes[0] = load_words_of("a_codes0", a_words, 0, PASSES)
-        load_rows_of("y", 1)
-        b_codes[0] = load_words_of("b_codes0", b_words, 0, PASSES)
-        load_scales_into(nc.sync, b_plane0, b_scales, 0, PASSES)
-        load_rows(2)
-        load_rows(3)
-        load_rows(4)
-        l_codes[0] = load_words_of("l_codes0", load_words, 0, 1)
-        load_scales_into(nc.sync, l_plane, load_scales, 0, G)
+        nc.sync.dma_start(out=gain_rows[:], in_=inv_var.rearrange("h (q j) -> (h q) j", j=G * N // P))
+        load_rows("x", 0)
+        load_rows("y", 0)
+        load_rows("x", 1)
+        a_codes[0] = load_codes("a_codes0", a_words, 0, PASSES)
+        load_rows("y", 1)
+        b_codes[0] = load_codes("b_codes0", b_words, 0, PASSES)
+        load_scale_rows(nc.sync, b_scales_first, b_scales, 0, PASSES)
+        for s in range(2, LOAD_AHEAD):
+            load_rows("x", s)
+            load_rows("y", s)
+        l_codes[0] = load_codes("l_codes0", load_words, 0, 1)
+        load_scale_rows(nc.sync, l_scales, load_scales, 0, G)
 
-        def load_group(h):
-            a_codes[h] = load_words_of("a_codes%d" % h, a_words, h * PASSES, PASSES)
-            b_codes[h] = load_words_of("b_codes%d" % h, b_words, h * PASSES, PASSES)
-            l_codes[h] = load_words_of("l_codes%d" % h, load_words, h, 1)
-
-        def stage1_scales(plane0, plane1, h, g):
-            return plane0[:, g, :] if h == 0 else plane1[:, (h - 1) * PASSES + g, :]
 
         gain = keep.tile([P, G, N], BF16, name="gain", align_bytes=64)
 
-        gain_banks = []
-
-        def spread_gain_turn():
+        def spread_gain():
             gain_words = gain_rows[:].bitcast(F32)
+            sorted_words = gain[:].bitcast(F32).rearrange("p h (u w) -> p h u w", u=2)
+            banks = []
             for u in range(2):
                 bank = sum_banks.tile([P, BANK], F32, name="sum_bank")
                 for c in range(4):
-                    j = 2 * c + u
-                    nc.tensor.transpose(
-                        bank[:, c * P : (c + 1) * P], gain_words[:, j : j + 1].to_broadcast([P, P]), ident[:]
-                    )
-                gain_banks.append(bank)
-
-        def spread_gain_copy():
-            sorted_words = gain[:].bitcast(F32).rearrange("p h (u w) -> p h u w", u=2)
-            for u, bank in enumerate(gain_banks):
+                    column = gain_words[:, 2 * c + u : 2 * c + u + 1].to_broadcast([P, P])
+                    nc.tensor.transpose(bank[:, c * P : (c + 1) * P], column, ident[:])
+                banks.append(bank)
+            for u in range(2):
                 nc.scalar.copy(
                     out=sorted_words[:, :, u, :].rearrange("p h (q c) -> p h q c", c=4),
-                    in_=bank[:].rearrange("p (c h q) -> p h q c", c=4, h=G),
+                    in_=banks[u][:].rearrange("p (c h q) -> p h q c", c=4, h=G),
                 )
 
-        pairs_sorted = {}
 
-        def sort_pairs(name, s):
-            width = len(steps[s]) * K
-            t = work.tile([P, width], BF16, name="sorted_" + name, align_bytes=64)
-            src = raw[name, s][:].rearrange("p j k -> p (j k)").rearrange("p (w u e) -> p u w e", u=2, e=2)
-            dst = t[:].rearrange("p (u w e) -> p u w e", u=2, e=2)
+        sorted_rows, turned, grouped, in_codes, in_scales, diff, squares = {}, {}, {}, {}, {}, {}, {}
+
+        def sort_words(name, s):
+            t = work.tile([P, len(steps[s]) * K], BF16, name="sorted_" + name, align_bytes=64)
+            rows = raw[name, s][:].rearrange("p j k -> p (j k)")
             if name == "x":
                 nc.vector.tensor_copy(
                     out=t[:].bitcast(F32).rearrange("p (u w) -> p u w", u=2),
-                    in_=raw[name, s][:].rearrange("p j k -> p (j k)").bitcast(F32).rearrange("p (w u) -> p u w", u=2),
+                    in_=rows.bitcast(F32).rearrange("p (w u) -> p u w", u=2),
                 )
             else:
-                nc.vector.tensor_scalar(out=dst, in0=src, scalar1=-1.0, scalar2=None, op0=ALU.mult)
-            pairs_sorted[name, s] = t
-
-        turned = {}
+                nc.vector.tensor_scalar(
+                    out=t[:].rearrange("p (u w e) -> p u w e", u=2, e=2),
+                    in0=rows.rearrange("p (w u e) -> p u w e", u=2, e=2),
+                    scalar1=-1.0,
+                    scalar2=None,
+                    op0=ALU.mult,
+                )
+            sorted_rows[name, s] = t
 
         def turn_inputs(i):
             s, j = step_of[i]
             for name in ("x", "y"):
-                words = pairs_sorted[name, s][:].bitcast(F32).rearrange("p (u w) -> p u w", u=2)
+                words = sorted_rows[name, s][:].bitcast(F32).rearrange("p (u w) -> p u w", u=2)
                 bank = turn_banks.tile([P, BANK], F32, name="turn_bank")
                 for g in range(PASSES):
                     for u in range(2):
@@ -179,212 +175,198 @@ def tile_grouped_alteration_detection_s14_kernel(
                         nc.tensor.transpose(bank[:, col : col + P], words[:, u, first : first + P], ident[:])
                 turned[name, i] = bank
 
-        def interleave(engine_copy, dst_bf16, bank):
-            engine_copy(
-                out=dst_bf16.bitcast(F32).rearrange("p (g m u) -> p g m u", u=2, m=P),
+        def interleave(copy, dst, bank):
+            copy(
+                out=dst.bitcast(F32).rearrange("p (g m u) -> p g m u", u=2, m=P),
                 in_=bank.rearrange("p (g u m) -> p g m u", u=2, m=P),
             )
 
-        grouped, in_codes, in_scales = {}, {}, {}
+        def copy_inputs(i, copy_x):
+            grouped[i] = work.tile([P, 2 * K], BF16, name="grouped", align_bytes=64)
+            interleave(copy_x, grouped[i][:, :K], turned["x", i][:])
+            interleave(on_scalar, grouped[i][:, K:], turned["y", i][:])
 
-        def copy_inputs(i):
-            t = work.tile([P, 2 * K], BF16, name="grouped", align_bytes=64)
-            interleave(nc.scalar.copy, t[:, :K], turned["x", i][:])
-            interleave(nc.vector.tensor_copy if i == 0 else nc.scalar.copy, t[:, K:], turned["y", i][:])
-            grouped[i] = t
-
-        def quantize_inputs(i):
-            c = work.tile([P, 2 * PASSES * P], U32, name="in_codes", bufs=4, align_bytes=64)
-            sc = work.tile([P, 2 * PASSES * P], U8, name="in_scales", bufs=4, align_bytes=64)
-            nc.vector.quantize_mx(out=c[:].bitcast(FP8X4), scales=sc[:], in_=grouped[i][:])
-            in_codes[i], in_scales[i] = c, sc
-
-        diff, squares = {}, {}
+        def quantize_inputs(i, parts):
+            in_codes[i] = work.tile([P, 2 * PASSES * P], U32, name="in_codes", bufs=4, align_bytes=64)
+            in_scales[i] = work.tile([P, 2 * PASSES * P], U8, name="in_scales", bufs=4, align_bytes=64)
+            width = 2 * PASSES * P // parts
+            for part in range(parts):
+                cols = slice(part * width, (part + 1) * width)
+                nc.vector.quantize_mx(
+                    out=in_codes[i][:, cols].bitcast(FP8X4),
+                    scales=in_scales[i][:, cols],
+                    in_=grouped[i][:, 4 * part * width : 4 * (part + 1) * width],
+                )
 
         def stage1(i):
             h = i // TILES_PER_GROUP
-            bank = sum_banks.tile([P, BANK], F32, name="sum_bank")
-            weights = [(a_codes[h], a_plane0, a_plane1), (b_codes[h], b_plane0, b_plane1)]
+            diff[i] = sum_banks.tile([P, BANK], F32, name="sum_bank")
+            weights = [(a_codes[h], a_scales_first, a_scales_rest), (b_codes[h], b_scales_first, b_scales_rest)]
             for c in range(2 * PASSES):
-                codes, plane0, plane1 = weights[c // PASSES]
+                codes, scales_first, scales_rest = weights[c // PASSES]
                 g = c % PASSES
                 cols = slice(c * P, (c + 1) * P)
                 nc.tensor.matmul_mx(
-                    out=bank[:],
+                    out=diff[i][:],
                     lhsT=in_codes[i][:, cols].bitcast(FP8X4),
                     lhsT_scale=in_scales[i][:, cols],
                     rhs=codes[:, g, :].bitcast(FP4X4),
-                    rhs_scale=stage1_scales(plane0, plane1, h, g),
+                    rhs_scale=scales_first[:, g, :] if h == 0 else scales_rest[:, (h - 1) * PASSES + g, :],
                     start=(c == 0),
                     stop=(c == 2 * PASSES - 1),
                 )
-            diff[i] = bank
 
         def square(i):
-            t = work.tile([P, N], F32, name="squares")
+            squares[i] = work.tile([P, N], F32, name="squares")
             nc.scalar.activation(
-                out=t[:].rearrange("p (u w e) -> p u w e", u=2, e=2),
+                out=squares[i][:].rearrange("p (u w e) -> p u w e", u=2, e=2),
                 in_=diff[i][:].rearrange("p (w u e) -> p u w e", u=2, e=2),
                 func=ACT.Square,
             )
-            squares[i] = t
 
-        z_rows, z_turned, z_grouped, z_codes, z_scales = {}, {}, {}, {}, {}
+
+        z_rows, z_turned, z_grouped, z_codes, z_scales, scores, results = {}, {}, {}, {}, {}, {}, {}
 
         def scale_squares(i):
-            t = work.tile([P, N], BF16, name="z_rows", bufs=4, align_bytes=64)
-            nc.vector.tensor_tensor(out=t[:], in0=squares[i][:], in1=gain[:, i // TILES_PER_GROUP, :], op=ALU.mult)
-            z_rows[i] = t
+            z_rows[i] = work.tile([P, N], BF16, name="z_rows", bufs=4, align_bytes=64)
+            nc.vector.tensor_tensor(
+                out=z_rows[i][:], in0=squares[i][:], in1=gain[:, i // TILES_PER_GROUP, :], op=ALU.mult
+            )
 
-        def turn_z(s):
-            bank = sum_banks.tile([P, BANK], F32, name="sum_bank")
-            for j, i in enumerate(units[s]):
+        def turn_z(z):
+            z_turned[z] = sum_banks.tile([P, BANK], F32, name="sum_bank")
+            for j, i in enumerate(batches[z]):
                 words = z_rows[i][:].bitcast(F32)
                 for u in range(2):
                     col = (j * 2 + u) * P
-                    nc.tensor.transpose(bank[:, col : col + P], words[:, u * P : (u + 1) * P], ident[:])
-            z_turned[s] = bank
+                    nc.tensor.transpose(z_turned[z][:, col : col + P], words[:, u * P : (u + 1) * P], z_ident[:])
 
-        def copy_z(s):
-            n = len(units[s])
-            t = work.tile([P, n * N], BF16, name="z_grouped", align_bytes=64)
-            interleave(nc.vector.tensor_copy, t[:], z_turned[s][:, : n * 2 * P])
-            z_grouped[s] = t
+        def copy_z(z):
+            count = len(batches[z])
+            z_grouped[z] = work.tile([P, count * N], BF16, name="z_grouped", align_bytes=64)
+            interleave(on_vector, z_grouped[z][:], z_turned[z][:, : count * 2 * P])
 
-        def quantize_z(s):
-            n = len(units[s])
-            c = work.tile([P, n * P], U32, name="z_codes", align_bytes=64)
-            sc = work.tile([P, n * P], U8, name="z_scales", align_bytes=64)
-            nc.vector.quantize_mx(out=c[:].bitcast(FP8X4), scales=sc[:], in_=z_grouped[s][:])
-            z_codes[s], z_scales[s] = c, sc
-
-        scores, results = {}, {}
+        def quantize_z(z):
+            count = len(batches[z])
+            z_codes[z] = work.tile([P, count * P], U32, name="z_codes", align_bytes=64)
+            z_scales[z] = work.tile([P, count * P], U8, name="z_scales", align_bytes=64)
+            nc.vector.quantize_mx(out=z_codes[z][:].bitcast(FP8X4), scales=z_scales[z][:], in_=z_grouped[z][:])
 
         def stage2(i):
-            s, j = unit_of[i]
+            z, j = batch_of[i]
             h = i // TILES_PER_GROUP
-            bank = sum_banks.tile([P, BANK], F32, name="sum_bank")
+            scores[i] = sum_banks.tile([P, BANK], F32, name="sum_bank")
             cols = slice(j * P, (j + 1) * P)
             nc.tensor.matmul_mx(
-                out=bank[:],
-                lhsT=z_codes[s][:, cols].bitcast(FP8X4),
-                lhsT_scale=z_scales[s][:, cols],
+                out=scores[i][:],
+                lhsT=z_codes[z][:, cols].bitcast(FP8X4),
+                lhsT_scale=z_scales[z][:, cols],
                 rhs=l_codes[h][:, 0, :].bitcast(FP4X4),
-                rhs_scale=l_plane[:, h, :],
+                rhs_scale=l_scales[:, h, :],
                 start=True,
                 stop=True,
             )
-            scores[i] = bank
 
         def copy_and_store(i, copy):
-            s, j = unit_of[i]
+            pair, j = divmod(i, 2)
             if j == 0:
-                results[s] = work.tile([P, len(units[s]), R], F32, name="result", bufs=4)
-            copy(out=results[s][:, j, :], in_=scores[i][:])
-            if i >= STORE1:
-                nc.sync.dma_start(out=rows_of(out, [i]), in_=results[s][:, j : j + 1, :])
-            elif j == len(units[s]) - 1:
-                nc.sync.dma_start(out=rows_of(out, units[s]), in_=results[s][:])
+                results[pair] = work.tile([P, 2, R], F32, name="result", bufs=4)
+            copy(out=results[pair][:, j, :], in_=scores[i][:])
+            if i >= SINGLE_STORES_FROM:
+                nc.sync.dma_start(out=rows_of(out, i, 1), in_=results[pair][:, j : j + 1, :])
+            elif j == 1:
+                nc.sync.dma_start(out=rows_of(out, i - 1, 2), in_=results[pair][:])
 
-        def load_ahead(s):
-            ahead = s + LOAD_AHEAD
-            if ahead < n_steps:
-                h, first = divmod(steps[ahead][0], TILES_PER_GROUP)
-                load_rows(ahead)
-                if first == 0:
-                    load_group(h)
-                    if h == 1:
-                        load_scales_into(nc.sync, a_plane1, a_scales, PASSES, (G - 1) * PASSES)
-                if first == 2 and h == 1:
-                    load_scales_into(nc.sync, b_plane1, b_scales, PASSES, (G - 1) * PASSES)
-
-        on_scalar, on_vector = nc.scalar.copy, nc.vector.tensor_copy
-
-        load_ahead(0)
-        sort_pairs("x", 0)
-        sort_pairs("y", 0)
+        preload_for(0)
+        spread_gain()
+        sort_words("x", 0)
+        sort_words("y", 0)
         turn_inputs(0)
-        spread_gain_turn()
-        sort_pairs("x", 1)
-        copy_inputs(0)
-        spread_gain_copy()
-        sort_pairs("y", 1)
-        quantize_inputs(0)
-        for s in range(1, SINGLES):
-            load_ahead(s)
+        sort_words("x", 1)
+        copy_inputs(0, on_vector)
+        sort_words("y", 1)
+        turn_inputs(1)
+        quantize_inputs(0, 2)
+        preload_for(1)
+        copy_inputs(1, on_scalar)
+        sort_words("x", 2)
+        sort_words("y", 2)
+        quantize_inputs(1, 1)
+        stage1(0)
+        square(0)
+
+        for s in range(2, SINGLE_STEPS):
+            preload_for(s)
             turn_inputs(s)
-            if s >= 2:
-                scale_squares(s - 2)
-            sort_pairs("x", s + 1)
-            sort_pairs("y", s + 1)
-            copy_inputs(s)
-            quantize_inputs(s)
+            sort_words("x", s + 1)
+            sort_words("y", s + 1)
+            scale_squares(s - 2)
+            copy_inputs(s, on_scalar)
+            quantize_inputs(s, 1)
             stage1(s - 1)
             square(s - 1)
 
-        last = n_steps - 1
-        for s in range(SINGLES, n_steps):
-            a, b = steps[s]
+        for s in range(SINGLE_STEPS, last_step + 1):
+            even, odd = steps[s]
             before = steps[s - 1]
-            unit = a // 2 - 2
-            load_ahead(s)
-            if s == SINGLES:
-                turn_z(unit)
-                copy_z(unit)
+            z = s - SINGLE_STEPS
+            preload_for(s)
+            turn_inputs(even)
+            if s < last_step:
+                sort_words("x", s + 1)
             scale_squares(before[0] - 1)
-            if s == SINGLES:
-                quantize_z(unit)
-            turn_inputs(a)
-            turn_inputs(b)
-            if s < last:
-                sort_pairs("x", s + 1)
-                sort_pairs("y", s + 1)
-            if s > SINGLES:
-                turn_z(unit)
-                copy_z(unit)
-            copy_inputs(a)
-            copy_inputs(b)
-            quantize_inputs(a)
-            if s > SINGLES:
-                quantize_z(unit)
-            quantize_inputs(b)
+            turn_z(z)
+            copy_z(z)
+            turn_inputs(odd)
+            if s < last_step:
+                sort_words("y", s + 1)
+            copy_inputs(even, on_scalar)
+            copy_inputs(odd, on_scalar)
+            if s < last_step:
+                quantize_z(z)
+                quantize_inputs(even, 1)
+            else:
+                quantize_inputs(even, 1)
+                quantize_z(z)
+            quantize_inputs(odd, 1)
             for i in before:
                 stage1(i)
                 square(i)
             for i in before[:-1]:
                 scale_squares(i)
-            if s < last + KEEP:
-                for i in units[unit]:
-                    stage2(i)
-                for i in units[unit]:
-                    copy_and_store(i, on_scalar)
+            for i in batches[z]:
+                stage2(i)
+            for i in batches[z]:
+                copy_and_store(i, on_scalar)
 
-        a, b = steps[last]
-        scale_squares(a - 1)
-        stage1(a)
-        square(a)
-        stage1(b)
-        turn_z(a // 2 - 1)
-        scale_squares(a)
-        copy_z(a // 2 - 1)
-        square(b)
-        stage2(a - 4)
-        stage2(a - 3)
-        turn_z(a // 2)
-        scale_squares(b)
-        quantize_z(a // 2 - 1)
-        copy_and_store(a - 4, on_scalar)
-        copy_and_store(a - 3, on_scalar)
-        copy_z(a // 2)
-        turn_z(a // 2 + 1)
-        stage2(a - 2)
-        stage2(a - 1)
-        copy_z(a // 2 + 1)
-        quantize_z(a // 2)
-        quantize_z(a // 2 + 1)
-        stage2(a)
-        stage2(b)
-        copy_and_store(a - 2, on_scalar)
-        copy_and_store(a - 1, on_vector)
-        copy_and_store(a, on_scalar)
-        copy_and_store(b, on_vector)
+        even, odd = steps[last_step]
+        z_pair, z_before, z_even, z_odd = range(len(batches) - 4, len(batches))
+        scale_squares(even - 1)
+        stage1(even)
+        square(even)
+        turn_z(z_pair)
+        copy_z(z_pair)
+        stage1(odd)
+        scale_squares(even)
+        quantize_z(z_pair)
+        square(odd)
+        turn_z(z_before)
+        turn_z(z_even)
+        copy_z(z_before)
+        scale_squares(odd)
+        stage2(even - 3)
+        stage2(even - 2)
+        quantize_z(z_before)
+        copy_z(z_even)
+        copy_and_store(even - 3, on_scalar)
+        turn_z(z_odd)
+        copy_and_store(even - 2, on_scalar)
+        quantize_z(z_even)
+        copy_z(z_odd)
+        stage2(even - 1)
+        stage2(even)
+        quantize_z(z_odd)
+        stage2(odd)
+        copy_and_store(even - 1, on_scalar)
+        copy_and_store(even, on_vector)
+        copy_and_store(odd, on_scalar)

@@ -24,7 +24,7 @@ TILES_PER_GROUP = M // P
 TILES = G * TILES_PER_GROUP
 SINGLE_STEPS = 4
 LOAD_AHEAD = 5
-SINGLE_STORES_FROM = TILES - 6
+SINGLE_STORES_FROM = TILES - 4
 
 
 def tile_grouped_alteration_detection_s14_kernel(
@@ -36,7 +36,7 @@ def tile_grouped_alteration_detection_s14_kernel(
     steps = [[i] for i in range(SINGLE_STEPS)] + [[i, i + 1] for i in range(SINGLE_STEPS, TILES, 2)]
     last_step = len(steps) - 1
     step_of = {i: (s, j) for s, tiles in enumerate(steps) for j, i in enumerate(tiles)}
-    batches = [[0]] + [[i, i + 1] for i in range(1, TILES - 3, 2)] + [[i] for i in range(TILES - 3, TILES)]
+    batches = [[i, i + 1] for i in range(0, TILES - 2, 2)] + [[TILES - 2], [TILES - 1]]
     batch_of = {i: (z, j) for z, tiles in enumerate(batches) for j, i in enumerate(tiles)}
 
     def rows_of(tensor, first_tile, count):
@@ -101,18 +101,18 @@ def tile_grouped_alteration_detection_s14_kernel(
         a_scales_rest = scale_tile("a_scales_rest", (G - 1) * PASSES)
         b_scales_rest = scale_tile("b_scales_rest", (G - 1) * PASSES)
 
-        ident = keep.tile([P, P], F32, name="ident")
-        make_identity(nc, ident[:])
+        eye = keep.tile([P, P], F32, name="eye")
+        make_identity(nc, eye[:])
 
         load_scale_rows(nc.scalar, a_scales_first, a_scales, 0, PASSES)
-        z_ident = keep.tile([P, P], F32, name="z_ident")
-        nc.scalar.activation(out=z_ident[:], in_=ident[:], func=ACT.Square)
+        ident = keep.tile([P, P], F32, name="ident")
+        nc.scalar.activation(out=ident[:], in_=eye[:], func=ACT.Square)
 
-        gain_rows = keep.tile([P, G * N // P], BF16, name="gain_rows")
-        nc.sync.dma_start(out=gain_rows[:], in_=inv_var.rearrange("h (q j) -> (h q) j", j=G * N // P))
         load_rows("x", 0)
         load_rows("y", 0)
         load_rows("x", 1)
+        gain_rows = keep.tile([P, G * N // P], BF16, name="gain_rows")
+        nc.sync.dma_start(out=gain_rows[:], in_=inv_var.rearrange("h (q j) -> (h q) j", j=G * N // P))
         a_codes[0] = load_codes("a_codes0", a_words, 0, PASSES)
         load_rows("y", 1)
         b_codes[0] = load_codes("b_codes0", b_words, 0, PASSES)
@@ -126,20 +126,23 @@ def tile_grouped_alteration_detection_s14_kernel(
 
         gain = keep.tile([P, G, N], BF16, name="gain", align_bytes=64)
 
-        def spread_gain():
+        gain_banks = []
+
+        def turn_gain():
             gain_words = gain_rows[:].bitcast(F32)
-            sorted_words = gain[:].bitcast(F32).rearrange("p h (u w) -> p h u w", u=2)
-            banks = []
             for u in range(2):
                 bank = sum_banks.tile([P, BANK], F32, name="sum_bank")
                 for c in range(4):
                     column = gain_words[:, 2 * c + u : 2 * c + u + 1].to_broadcast([P, P])
                     nc.tensor.transpose(bank[:, c * P : (c + 1) * P], column, ident[:])
-                banks.append(bank)
+                gain_banks.append(bank)
+
+        def copy_gain():
+            sorted_words = gain[:].bitcast(F32).rearrange("p h (u w) -> p h u w", u=2)
             for u in range(2):
                 nc.scalar.copy(
                     out=sorted_words[:, :, u, :].rearrange("p h (q c) -> p h q c", c=4),
-                    in_=banks[u][:].rearrange("p (c h q) -> p h q c", c=4, h=G),
+                    in_=gain_banks[u][:].rearrange("p (c h q) -> p h q c", c=4, h=G),
                 )
 
 
@@ -150,13 +153,13 @@ def tile_grouped_alteration_detection_s14_kernel(
             rows = raw[name, s][:].rearrange("p j k -> p (j k)")
             if name == "x":
                 nc.vector.tensor_copy(
-                    out=t[:].bitcast(F32).rearrange("p (u w) -> p u w", u=2),
-                    in_=rows.bitcast(F32).rearrange("p (w u) -> p u w", u=2),
+                    out=t[:].bitcast(F32).rearrange("p (u c i) -> p c u i", u=2, i=2),
+                    in_=rows.bitcast(F32).rearrange("p (c i u) -> p c u i", u=2, i=2),
                 )
             else:
                 nc.vector.tensor_scalar(
-                    out=t[:].rearrange("p (u w e) -> p u w e", u=2, e=2),
-                    in0=rows.rearrange("p (w u e) -> p u w e", u=2, e=2),
+                    out=t[:].rearrange("p (u w e) -> p w u e", u=2, e=2),
+                    in0=rows.rearrange("p (w u e) -> p w u e", u=2, e=2),
                     scalar1=-1.0,
                     scalar2=None,
                     op0=ALU.mult,
@@ -181,22 +184,15 @@ def tile_grouped_alteration_detection_s14_kernel(
                 in_=bank.rearrange("p (g u m) -> p g m u", u=2, m=P),
             )
 
-        def copy_inputs(i, copy_x):
+        def copy_inputs(i, copy_y):
             grouped[i] = work.tile([P, 2 * K], BF16, name="grouped", align_bytes=64)
-            interleave(copy_x, grouped[i][:, :K], turned["x", i][:])
-            interleave(on_scalar, grouped[i][:, K:], turned["y", i][:])
+            interleave(on_scalar, grouped[i][:, :K], turned["x", i][:])
+            interleave(copy_y, grouped[i][:, K:], turned["y", i][:])
 
-        def quantize_inputs(i, parts):
+        def quantize_inputs(i):
             in_codes[i] = work.tile([P, 2 * PASSES * P], U32, name="in_codes", bufs=4, align_bytes=64)
             in_scales[i] = work.tile([P, 2 * PASSES * P], U8, name="in_scales", bufs=4, align_bytes=64)
-            width = 2 * PASSES * P // parts
-            for part in range(parts):
-                cols = slice(part * width, (part + 1) * width)
-                nc.vector.quantize_mx(
-                    out=in_codes[i][:, cols].bitcast(FP8X4),
-                    scales=in_scales[i][:, cols],
-                    in_=grouped[i][:, 4 * part * width : 4 * (part + 1) * width],
-                )
+            nc.vector.quantize_mx(out=in_codes[i][:].bitcast(FP8X4), scales=in_scales[i][:], in_=grouped[i][:])
 
         def stage1(i):
             h = i // TILES_PER_GROUP
@@ -239,7 +235,7 @@ def tile_grouped_alteration_detection_s14_kernel(
                 words = z_rows[i][:].bitcast(F32)
                 for u in range(2):
                     col = (j * 2 + u) * P
-                    nc.tensor.transpose(z_turned[z][:, col : col + P], words[:, u * P : (u + 1) * P], z_ident[:])
+                    nc.tensor.transpose(z_turned[z][:, col : col + P], words[:, u * P : (u + 1) * P], ident[:])
 
         def copy_z(z):
             count = len(batches[z])
@@ -268,41 +264,35 @@ def tile_grouped_alteration_detection_s14_kernel(
             )
 
         def copy_and_store(i, copy):
-            pair, j = divmod(i, 2)
+            z, j = batch_of[i]
             if j == 0:
-                results[pair] = work.tile([P, 2, R], F32, name="result", bufs=4)
-            copy(out=results[pair][:, j, :], in_=scores[i][:])
+                results[z] = work.tile([P, len(batches[z]), R], F32, name="result", bufs=4)
+            copy(out=results[z][:, j, :], in_=scores[i][:])
             if i >= SINGLE_STORES_FROM:
-                nc.sync.dma_start(out=rows_of(out, i, 1), in_=results[pair][:, j : j + 1, :])
+                nc.sync.dma_start(out=rows_of(out, i, 1), in_=results[z][:, j : j + 1, :])
             elif j == 1:
-                nc.sync.dma_start(out=rows_of(out, i - 1, 2), in_=results[pair][:])
+                nc.sync.dma_start(out=rows_of(out, i - 1, 2), in_=results[z][:])
 
         preload_for(0)
-        spread_gain()
         sort_words("x", 0)
         sort_words("y", 0)
         turn_inputs(0)
+        turn_gain()
         sort_words("x", 1)
         copy_inputs(0, on_vector)
+        copy_gain()
         sort_words("y", 1)
-        turn_inputs(1)
-        quantize_inputs(0, 2)
-        preload_for(1)
-        copy_inputs(1, on_scalar)
-        sort_words("x", 2)
-        sort_words("y", 2)
-        quantize_inputs(1, 1)
-        stage1(0)
-        square(0)
+        quantize_inputs(0)
 
-        for s in range(2, SINGLE_STEPS):
+        for s in range(1, SINGLE_STEPS):
             preload_for(s)
             turn_inputs(s)
+            if s >= 2:
+                scale_squares(s - 2)
             sort_words("x", s + 1)
             sort_words("y", s + 1)
-            scale_squares(s - 2)
             copy_inputs(s, on_scalar)
-            quantize_inputs(s, 1)
+            quantize_inputs(s)
             stage1(s - 1)
             square(s - 1)
 
@@ -310,63 +300,64 @@ def tile_grouped_alteration_detection_s14_kernel(
             even, odd = steps[s]
             before = steps[s - 1]
             z = s - SINGLE_STEPS
+            z_first = s == SINGLE_STEPS
             preload_for(s)
-            turn_inputs(even)
-            if s < last_step:
-                sort_words("x", s + 1)
+            if z_first:
+                turn_z(z)
+                copy_z(z)
             scale_squares(before[0] - 1)
-            turn_z(z)
-            copy_z(z)
+            if z_first:
+                quantize_z(z)
+            turn_inputs(even)
             turn_inputs(odd)
             if s < last_step:
+                sort_words("x", s + 1)
                 sort_words("y", s + 1)
+            if not z_first:
+                turn_z(z)
+                copy_z(z)
             copy_inputs(even, on_scalar)
             copy_inputs(odd, on_scalar)
-            if s < last_step:
+            quantize_inputs(even)
+            if not z_first:
                 quantize_z(z)
-                quantize_inputs(even, 1)
-            else:
-                quantize_inputs(even, 1)
-                quantize_z(z)
-            quantize_inputs(odd, 1)
+            quantize_inputs(odd)
             for i in before:
                 stage1(i)
                 square(i)
             for i in before[:-1]:
                 scale_squares(i)
-            for i in batches[z]:
-                stage2(i)
-            for i in batches[z]:
-                copy_and_store(i, on_scalar)
+            if s < last_step:
+                for i in batches[z]:
+                    stage2(i)
+                for i in batches[z]:
+                    copy_and_store(i, on_scalar)
 
         even, odd = steps[last_step]
-        z_pair, z_before, z_even, z_odd = range(len(batches) - 4, len(batches))
+        z_quantised, z_pair, z_even, z_odd = range(len(batches) - 4, len(batches))
         scale_squares(even - 1)
         stage1(even)
         square(even)
-        turn_z(z_pair)
-        copy_z(z_pair)
         stage1(odd)
+        turn_z(z_pair)
         scale_squares(even)
-        quantize_z(z_pair)
+        copy_z(z_pair)
         square(odd)
-        turn_z(z_before)
+        for i in batches[z_quantised]:
+            stage2(i)
         turn_z(z_even)
-        copy_z(z_before)
         scale_squares(odd)
-        stage2(even - 3)
-        stage2(even - 2)
-        quantize_z(z_before)
+        quantize_z(z_pair)
+        for i in batches[z_quantised]:
+            copy_and_store(i, on_scalar)
         copy_z(z_even)
-        copy_and_store(even - 3, on_scalar)
         turn_z(z_odd)
-        copy_and_store(even - 2, on_scalar)
-        quantize_z(z_even)
+        for i in batches[z_pair]:
+            stage2(i)
         copy_z(z_odd)
-        stage2(even - 1)
-        stage2(even)
+        quantize_z(z_even)
         quantize_z(z_odd)
+        stage2(even)
         stage2(odd)
-        copy_and_store(even - 1, on_scalar)
-        copy_and_store(even, on_vector)
-        copy_and_store(odd, on_scalar)
+        for i in range(even - 2, TILES):
+            copy_and_store(i, on_vector if i % 2 else on_scalar)

from contextlib import ExitStack

import concourse.mybir as mybir
from concourse.masks import make_identity

G, M, K, N, R = 4, 768, 1024, 512, 512
FLOPS = G * (2 * 2 * M * K * N + 2 * M * N * R)

F32 = mybir.dt.float32
BF16 = mybir.dt.bfloat16
I32 = mybir.dt.int32
U32 = mybir.dt.uint32
U8 = mybir.dt.uint8
FP8X4 = mybir.dt.float8_e4m3fn_x4
FP4X4 = mybir.dt.float4_e2m1fn_x4
ALU = mybir.AluOpType
ACT = mybir.ActivationFunctionType

P = 128
K_PASS = 512
PASSES = K // K_PASS
BANK = 512
TILES_PER_GROUP = M // P
TILES = G * TILES_PER_GROUP
SINGLE_STEPS = 4
LOAD_AHEAD = 5
SINGLE_STORES_FROM = TILES - 4


def tile_grouped_alteration_detection_s14_kernel(
    tc, x, y, inv_var, a_words, a_scales, b_words, b_scales, load_words, load_scales, out
):
    nc = tc.nc
    on_scalar, on_vector = nc.scalar.copy, nc.vector.tensor_copy

    steps = [[i] for i in range(SINGLE_STEPS)] + [[i, i + 1] for i in range(SINGLE_STEPS, TILES, 2)]
    last_step = len(steps) - 1
    step_of = {i: (s, j) for s, tiles in enumerate(steps) for j, i in enumerate(tiles)}
    batches = [[i, i + 1] for i in range(0, TILES - 2, 2)] + [[TILES - 2], [TILES - 1]]
    batch_of = {i: (z, j) for z, tiles in enumerate(batches) for j, i in enumerate(tiles)}

    def rows_of(tensor, first_tile, count):
        h, in_group = divmod(first_tile, TILES_PER_GROUP)
        pair, j = divmod(in_group, 2)
        rows = tensor[h, 2 * P * pair : 2 * P * (pair + 1), :].rearrange("(p j) c -> p j c", j=2)
        return rows[:, j : j + count, :]

    with ExitStack() as ctx:
        keep = ctx.enter_context(tc.tile_pool(name="keep", bufs=1))
        raw_pool = ctx.enter_context(tc.tile_pool(name="raw", bufs=LOAD_AHEAD + 1))
        work = ctx.enter_context(tc.tile_pool(name="work", bufs=3))
        turn_banks = ctx.enter_context(tc.psum_pool(name="turn_banks", bufs=4))
        sum_banks = ctx.enter_context(tc.psum_pool(name="sum_banks", bufs=4))
        ctx.enter_context(tc.manual_schedule())


        def scale_tile(name, passes):
            t = keep.tile([P, passes, N], U8, name=name, align_bytes=64)
            nc.vector.memset(t[:].bitcast(I32), 0)
            return t

        def load_scale_rows(queue, t, scales, first_pass, passes):
            for q in range(4):
                rows = scales[first_pass : first_pass + passes, 4 * q : 4 * q + 4, :]
                queue.dma_start(
                    out=t[32 * q : 32 * q + 4, :, :].bitcast(I32), in_=rows.rearrange("g r n -> r g n").bitcast(I32)
                )

        def load_codes(name, words, first_pass, passes):
            t = keep.tile([P, passes, 2 * N], U8, name=name, align_bytes=64)
            rows = words[first_pass : first_pass + passes, :, :]
            nc.sync.dma_start(out=t[:].bitcast(I32), in_=rows.rearrange("g p b -> p g b").bitcast(I32))
            return t

        raw, a_codes, b_codes, l_codes = {}, {}, {}, {}

        def load_rows(name, s):
            count = len(steps[s])
            raw[name, s] = raw_pool.tile([P, count, K], BF16, name="raw_" + name, align_bytes=64)
            nc.sync.dma_start(out=raw[name, s][:], in_=rows_of(x if name == "x" else y, steps[s][0], count))

        def preload_for(s):
            ahead = s + LOAD_AHEAD
            if ahead > last_step:
                return
            load_rows("x", ahead)
            load_rows("y", ahead)
            h, in_group = divmod(steps[ahead][0], TILES_PER_GROUP)
            if in_group == 0:
                a_codes[h] = load_codes("a_codes%d" % h, a_words, h * PASSES, PASSES)
                b_codes[h] = load_codes("b_codes%d" % h, b_words, h * PASSES, PASSES)
                l_codes[h] = load_codes("l_codes%d" % h, load_words, h, 1)
            if steps[ahead][0] == TILES_PER_GROUP:
                load_scale_rows(nc.sync, a_scales_rest, a_scales, PASSES, (G - 1) * PASSES)
            if steps[ahead][0] == TILES_PER_GROUP + 2:
                load_scale_rows(nc.sync, b_scales_rest, b_scales, PASSES, (G - 1) * PASSES)

        a_scales_first = scale_tile("a_scales_first", PASSES)
        b_scales_first = scale_tile("b_scales_first", PASSES)
        l_scales = scale_tile("l_scales", G)
        a_scales_rest = scale_tile("a_scales_rest", (G - 1) * PASSES)
        b_scales_rest = scale_tile("b_scales_rest", (G - 1) * PASSES)

        eye = keep.tile([P, P], F32, name="eye")
        make_identity(nc, eye[:])

        load_scale_rows(nc.scalar, a_scales_first, a_scales, 0, PASSES)
        ident = keep.tile([P, P], F32, name="ident")
        nc.scalar.activation(out=ident[:], in_=eye[:], func=ACT.Square)

        load_rows("x", 0)
        load_rows("y", 0)
        load_rows("x", 1)
        gain_rows = keep.tile([P, G * N // P], BF16, name="gain_rows")
        nc.sync.dma_start(out=gain_rows[:], in_=inv_var.rearrange("h (q j) -> (h q) j", j=G * N // P))
        a_codes[0] = load_codes("a_codes0", a_words, 0, PASSES)
        load_rows("y", 1)
        b_codes[0] = load_codes("b_codes0", b_words, 0, PASSES)
        load_scale_rows(nc.sync, b_scales_first, b_scales, 0, PASSES)
        for s in range(2, LOAD_AHEAD):
            load_rows("x", s)
            load_rows("y", s)
        l_codes[0] = load_codes("l_codes0", load_words, 0, 1)
        load_scale_rows(nc.sync, l_scales, load_scales, 0, G)


        gain = keep.tile([P, G, N], BF16, name="gain", align_bytes=64)

        gain_banks = []

        def turn_gain():
            gain_words = gain_rows[:].bitcast(F32)
            for u in range(2):
                bank = sum_banks.tile([P, BANK], F32, name="sum_bank")
                for c in range(4):
                    column = gain_words[:, 2 * c + u : 2 * c + u + 1].to_broadcast([P, P])
                    nc.tensor.transpose(bank[:, c * P : (c + 1) * P], column, ident[:])
                gain_banks.append(bank)

        def copy_gain():
            sorted_words = gain[:].bitcast(F32).rearrange("p h (u w) -> p h u w", u=2)
            for u in range(2):
                nc.scalar.copy(
                    out=sorted_words[:, :, u, :].rearrange("p h (q c) -> p h q c", c=4),
                    in_=gain_banks[u][:].rearrange("p (c h q) -> p h q c", c=4, h=G),
                )


        sorted_rows, turned, grouped, in_codes, in_scales, diff, squares = {}, {}, {}, {}, {}, {}, {}

        def sort_words(name, s):
            t = work.tile([P, len(steps[s]) * K], BF16, name="sorted_" + name, align_bytes=64)
            rows = raw[name, s][:].rearrange("p j k -> p (j k)")
            if name == "x":
                nc.vector.tensor_copy(
                    out=t[:].bitcast(F32).rearrange("p (u c i) -> p c u i", u=2, i=2),
                    in_=rows.bitcast(F32).rearrange("p (c i u) -> p c u i", u=2, i=2),
                )
            else:
                nc.vector.tensor_scalar(
                    out=t[:].rearrange("p (u w e) -> p w u e", u=2, e=2),
                    in0=rows.rearrange("p (w u e) -> p w u e", u=2, e=2),
                    scalar1=-1.0,
                    scalar2=None,
                    op0=ALU.mult,
                )
            sorted_rows[name, s] = t

        def turn_inputs(i):
            s, j = step_of[i]
            for name in ("x", "y"):
                words = sorted_rows[name, s][:].bitcast(F32).rearrange("p (u w) -> p u w", u=2)
                bank = turn_banks.tile([P, BANK], F32, name="turn_bank")
                for g in range(PASSES):
                    for u in range(2):
                        first = (j * PASSES + g) * P
                        col = (g * 2 + u) * P
                        nc.tensor.transpose(bank[:, col : col + P], words[:, u, first : first + P], ident[:])
                turned[name, i] = bank

        def interleave(copy, dst, bank):
            copy(
                out=dst.bitcast(F32).rearrange("p (g m u) -> p g m u", u=2, m=P),
                in_=bank.rearrange("p (g u m) -> p g m u", u=2, m=P),
            )

        def copy_inputs(i, copy_y):
            grouped[i] = work.tile([P, 2 * K], BF16, name="grouped", align_bytes=64)
            interleave(on_scalar, grouped[i][:, :K], turned["x", i][:])
            interleave(copy_y, grouped[i][:, K:], turned["y", i][:])

        def quantize_inputs(i):
            in_codes[i] = work.tile([P, 2 * PASSES * P], U32, name="in_codes", bufs=4, align_bytes=64)
            in_scales[i] = work.tile([P, 2 * PASSES * P], U8, name="in_scales", bufs=4, align_bytes=64)
            nc.vector.quantize_mx(out=in_codes[i][:].bitcast(FP8X4), scales=in_scales[i][:], in_=grouped[i][:])

        def stage1(i):
            h = i // TILES_PER_GROUP
            diff[i] = sum_banks.tile([P, BANK], F32, name="sum_bank")
            weights = [(a_codes[h], a_scales_first, a_scales_rest), (b_codes[h], b_scales_first, b_scales_rest)]
            for c in range(2 * PASSES):
                codes, scales_first, scales_rest = weights[c // PASSES]
                g = c % PASSES
                cols = slice(c * P, (c + 1) * P)
                nc.tensor.matmul_mx(
                    out=diff[i][:],
                    lhsT=in_codes[i][:, cols].bitcast(FP8X4),
                    lhsT_scale=in_scales[i][:, cols],
                    rhs=codes[:, g, :].bitcast(FP4X4),
                    rhs_scale=scales_first[:, g, :] if h == 0 else scales_rest[:, (h - 1) * PASSES + g, :],
                    start=(c == 0),
                    stop=(c == 2 * PASSES - 1),
                )

        def square(i):
            squares[i] = work.tile([P, N], F32, name="squares")
            nc.scalar.activation(
                out=squares[i][:].rearrange("p (u w e) -> p u w e", u=2, e=2),
                in_=diff[i][:].rearrange("p (w u e) -> p u w e", u=2, e=2),
                func=ACT.Square,
            )


        z_rows, z_turned, z_grouped, z_codes, z_scales, scores, results = {}, {}, {}, {}, {}, {}, {}

        def scale_squares(i):
            z_rows[i] = work.tile([P, N], BF16, name="z_rows", bufs=4, align_bytes=64)
            nc.vector.tensor_tensor(
                out=z_rows[i][:], in0=squares[i][:], in1=gain[:, i // TILES_PER_GROUP, :], op=ALU.mult
            )

        def turn_z(z):
            z_turned[z] = sum_banks.tile([P, BANK], F32, name="sum_bank")
            for j, i in enumerate(batches[z]):
                words = z_rows[i][:].bitcast(F32)
                for u in range(2):
                    col = (j * 2 + u) * P
                    nc.tensor.transpose(z_turned[z][:, col : col + P], words[:, u * P : (u + 1) * P], ident[:])

        def copy_z(z):
            count = len(batches[z])
            z_grouped[z] = work.tile([P, count * N], BF16, name="z_grouped", align_bytes=64)
            interleave(on_vector, z_grouped[z][:], z_turned[z][:, : count * 2 * P])

        def quantize_z(z):
            count = len(batches[z])
            z_codes[z] = work.tile([P, count * P], U32, name="z_codes", align_bytes=64)
            z_scales[z] = work.tile([P, count * P], U8, name="z_scales", align_bytes=64)
            nc.vector.quantize_mx(out=z_codes[z][:].bitcast(FP8X4), scales=z_scales[z][:], in_=z_grouped[z][:])

        def stage2(i):
            z, j = batch_of[i]
            h = i // TILES_PER_GROUP
            scores[i] = sum_banks.tile([P, BANK], F32, name="sum_bank")
            cols = slice(j * P, (j + 1) * P)
            nc.tensor.matmul_mx(
                out=scores[i][:],
                lhsT=z_codes[z][:, cols].bitcast(FP8X4),
                lhsT_scale=z_scales[z][:, cols],
                rhs=l_codes[h][:, 0, :].bitcast(FP4X4),
                rhs_scale=l_scales[:, h, :],
                start=True,
                stop=True,
            )

        def copy_and_store(i, copy):
            z, j = batch_of[i]
            if j == 0:
                results[z] = work.tile([P, len(batches[z]), R], F32, name="result", bufs=4)
            copy(out=results[z][:, j, :], in_=scores[i][:])
            if i >= SINGLE_STORES_FROM:
                nc.sync.dma_start(out=rows_of(out, i, 1), in_=results[z][:, j : j + 1, :])
            elif j == 1:
                nc.sync.dma_start(out=rows_of(out, i - 1, 2), in_=results[z][:])

        preload_for(0)
        sort_words("x", 0)
        sort_words("y", 0)
        turn_inputs(0)
        turn_gain()
        sort_words("x", 1)
        copy_inputs(0, on_vector)
        copy_gain()
        sort_words("y", 1)
        quantize_inputs(0)

        for s in range(1, SINGLE_STEPS):
            preload_for(s)
            turn_inputs(s)
            if s >= 2:
                scale_squares(s - 2)
            sort_words("x", s + 1)
            sort_words("y", s + 1)
            copy_inputs(s, on_scalar)
            quantize_inputs(s)
            stage1(s - 1)
            square(s - 1)

        for s in range(SINGLE_STEPS, last_step + 1):
            even, odd = steps[s]
            before = steps[s - 1]
            z = s - SINGLE_STEPS
            z_first = s == SINGLE_STEPS
            preload_for(s)
            if z_first:
                turn_z(z)
                copy_z(z)
            scale_squares(before[0] - 1)
            if z_first:
                quantize_z(z)
            turn_inputs(even)
            turn_inputs(odd)
            if s < last_step:
                sort_words("x", s + 1)
                sort_words("y", s + 1)
            if not z_first:
                turn_z(z)
                copy_z(z)
            copy_inputs(even, on_scalar)
            copy_inputs(odd, on_scalar)
            quantize_inputs(even)
            if not z_first:
                quantize_z(z)
            quantize_inputs(odd)
            for i in before:
                stage1(i)
                square(i)
            for i in before[:-1]:
                scale_squares(i)
            if s < last_step:
                for i in batches[z]:
                    stage2(i)
                for i in batches[z]:
                    copy_and_store(i, on_scalar)

        even, odd = steps[last_step]
        z_quantised, z_pair, z_even, z_odd = range(len(batches) - 4, len(batches))
        scale_squares(even - 1)
        stage1(even)
        square(even)
        stage1(odd)
        turn_z(z_pair)
        scale_squares(even)
        copy_z(z_pair)
        square(odd)
        for i in batches[z_quantised]:
            stage2(i)
        turn_z(z_even)
        scale_squares(odd)
        quantize_z(z_pair)
        for i in batches[z_quantised]:
            copy_and_store(i, on_scalar)
        copy_z(z_even)
        turn_z(z_odd)
        for i in batches[z_pair]:
            stage2(i)
        copy_z(z_odd)
        quantize_z(z_even)
        quantize_z(z_odd)
        stage2(even)
        stage2(odd)
        for i in range(even - 2, TILES):
            copy_and_store(i, on_vector if i % 2 else on_scalar)
